import numpy as np
import ml_dtypes


def mxq(x, axis, fmt="e4m3"):
    dtype, down = {"e4m3": (ml_dtypes.float8_e4m3fn, 7), "e5m2": (ml_dtypes.float8_e5m2, 14)}[fmt]
    v = np.moveaxis(np.asarray(x, np.float32).astype(ml_dtypes.bfloat16).astype(np.float64), axis, -1)
    blocks = v.reshape(v.shape[:-1] + (-1, 32))
    amax = np.abs(blocks).max(-1, keepdims=True)
    byte = np.maximum(np.where(amax > 0, np.frexp(amax)[1] - 1 + 127, 0) - down, 1)
    scale = np.exp2(byte - 127.0)
    codes = (blocks / scale).astype(np.float32).astype(dtype).astype(np.float64)
    return np.moveaxis((codes * scale).reshape(v.shape), -1, axis)


WIDE = False


def mx_kscale(k):
    if not WIDE:
        return np.ones(k)
    levels = np.array([10, -10, 5, -5, 0])
    if k % 512:
        return np.exp2(np.random.permutation(np.resize(levels, k // 32))).repeat(32)
    a = np.empty((k // 512, 16))
    for p in range(k // 512):
        a[p, :8] = np.random.permutation(np.resize(levels, 8))
        for g in range(8):
            far = levels[np.abs(levels - a[p, g]) >= 10]
            a[p, g + 8] = far[np.random.randint(len(far))]
    return np.exp2(a.ravel()).repeat(32)


BF16 = ml_dtypes.bfloat16


def bf(x):
    return np.asarray(x, np.float32).astype(BF16)


def f64(x):
    return np.asarray(x).astype(np.float64)


E2M1 = np.array([0.0, 0.5, 1.0, 1.5, 2.0, 3.0, 4.0, 6.0, -0.0, -0.5, -1.0, -1.5, -2.0, -3.0, -4.0, -6.0])


def pack_weight(w, fmt):
    k, n = w.shape
    w = f64(bf(w)).reshape(k // 32, 32, n)
    amax = np.abs(w).max(1)
    if fmt == "e4m3":
        byte = np.frexp(amax)[1] - 1 + 127 - 7
    else:
        mant, ex = np.frexp(amax / 6.0)
        byte = np.where(mant > 0.5, ex, ex - 1) + 127
    byte = np.clip(np.where(amax > 0, byte, 1), 1, 254)
    scaled = (w * np.exp2(127.0 - byte)[:, None, :]).reshape(k, n).astype(np.float32)
    by_word = np.ascontiguousarray(scaled.reshape(k // 512, 128, 4, n).transpose(0, 1, 3, 2))
    if fmt == "e4m3":
        words = by_word.astype(ml_dtypes.float8_e4m3fn).view(np.uint8)
    else:
        c = by_word.astype(ml_dtypes.float4_e2m1fn).view(np.uint8) & 0xF
        words = c[..., 0::2] | (c[..., 1::2] << 4)
    return np.ascontiguousarray(words), np.ascontiguousarray(byte.astype(np.uint8).reshape(k // 512, 16, n))


def unpack_weight(words, scales, fmt):
    g, p, n, _ = words.shape
    if fmt == "e4m3":
        vals = np.ascontiguousarray(words).view(ml_dtypes.float8_e4m3fn).astype(np.float64)
    else:
        nib = np.empty((g, p, n, 4), np.uint8)
        nib[..., 0::2] = words & 0xF
        nib[..., 1::2] = words >> 4
        vals = E2M1[nib]
    vals = vals * np.repeat(np.exp2(scales.astype(np.float64) - 127.0), 8, axis=1)[..., None]
    return vals.transpose(0, 1, 3, 2).reshape(g * 512, n)


E, K, D, C, NB = 256, 16, 512, 128, 8
NBC = NB * C


def silu(v):
    return v / (1.0 + np.exp(-v))


def draw0():
    s = mx_kscale(D)
    t = mx_kscale(NBC)
    m_kj = bf(np.random.standard_normal((E, K, D)) * s)
    m_ji = bf(np.random.standard_normal((E, D)))
    sbf = bf(np.random.standard_normal((E, K, NB)))
    w_down_words, w_down_scales = pack_weight(np.random.standard_normal((D, C)) / np.sqrt(D) / s[:, None], "e4m3")
    gain = bf((1.0 + 0.1 * np.random.standard_normal(NBC)) * t)
    w_bil_words, w_bil_scales = pack_weight(np.random.standard_normal((NBC, D)) * 2.0 / np.sqrt(NBC) / t[:, None], "e4m3")
    return {"m_kj": m_kj, "m_ji": m_ji, "sbf": sbf, "w_down_words": w_down_words, "w_down_scales": w_down_scales, "gain": gain, "w_bil_words": w_bil_words, "w_bil_scales": w_bil_scales}


def core(m_kj, m_ji, sbf, w_down_words, w_down_scales, gain, w_bil_words, w_bil_scales):
    m_kj, m_ji, sbf, gain = f64(m_kj), f64(m_ji), f64(sbf), f64(gain)
    e, k, _ = m_kj.shape
    nbc = gain.shape[0]
    x = silu(mxq(m_kj, 2, "e4m3") @ unpack_weight(w_down_words, w_down_scales, "e4m3"))
    q = (sbf[:, :, :, None] * x[:, :, None, :]).reshape(e, k, nbc)
    p = q * gain
    t = silu(mxq(p, 2, "e4m3") @ unpack_weight(w_bil_words, w_bil_scales, "e4m3"))
    agg = np.sum(t, axis=1) / np.sqrt(k)
    return m_ji + agg


def e4m3fn_bytes(y):
    return np.clip(np.asarray(y, np.float64), -448.0, 448.0).astype(np.float32).astype(ml_dtypes.float8_e4m3fn).view(np.uint8)


def e4m3fn_values(b):
    return np.asarray(b, np.uint8).view(ml_dtypes.float8_e4m3fn).astype(np.float64)


def setup_inputs():
    d = draw0()
    x0 = np.asarray(d['m_kj']).astype(np.float64)
    s = (np.max(np.abs(x0), axis=(0, 1), keepdims=True) / 448.0).astype(np.float32)
    out = {}
    for k, v in d.items():
        if k == 'm_kj':
            out['m_kj_bytes'] = e4m3fn_bytes(x0 / s.astype(np.float64))
            out['m_kj_scale'] = s
        else:
            out[k] = v
    return out


def reference(m_kj_bytes, m_kj_scale, m_ji, sbf, w_down_words, w_down_scales, gain, w_bil_words, w_bil_scales):
    return core(e4m3fn_values(m_kj_bytes) * m_kj_scale.astype(np.float64), m_ji, sbf, w_down_words, w_down_scales, gain, w_bil_words, w_bil_scales)

@@ -1,0 +1,309 @@
+from contextlib import ExitStack
+
+import concourse.mybir as mybir
+from concourse.masks import make_identity
+
+F32 = mybir.dt.float32
+BF16 = mybir.dt.bfloat16
+I32 = mybir.dt.int32
+U8 = mybir.dt.uint8
+FP8 = mybir.dt.float8_e4m3fn
+FP8X4 = mybir.dt.float8_e4m3fn_x4
+ACT = mybir.ActivationFunctionType
+ALU = mybir.AluOpType
+
+P = 128
+E, K, D, C, NB = 256, 16, 512, 128, 8
+NBC = NB * C
+FLOPS = 2 * E * K * D * C + 2 * E * K * NBC * D
+PAIRS = E * K // P // 2
+PPB = K // 2
+
+
+def tile_dimenettripletbilinear_w8_kernel(
+    tc, m_kj_bytes, m_kj_scale, m_ji, sbf, w_down_words, w_down_scales, gain, w_bil_words, w_bil_scales, out
+):
+    nc = tc.nc
+    with ExitStack() as ctx:
+        keep = ctx.enter_context(tc.tile_pool(name="keep", bufs=1))
+        work = ctx.enter_context(tc.tile_pool(name="work", bufs=3))
+        psum = ctx.enter_context(tc.psum_pool(name="psum", bufs=1))
+        ctx.enter_context(tc.manual_schedule())
+
+        chunk_k = [2, 2, 4, 4, 4, 4, 4, 4, 4]
+        raws = []
+        where = {}
+        pos = 0
+        for ci, nk in enumerate(chunk_k):
+            raw = keep.tile([P, nk * D], U8, name="raw%d" % ci, align_bytes=64)
+            raws.append((raw, pos, nk))
+            for j in range(nk):
+                where[pos + j] = (raw, j)
+            pos += nk
+
+        def load_raw(ci):
+            raw, p0, nk = raws[ci]
+            b, k0 = divmod(p0, K)
+            nc.sync.dma_start(
+                out=raw[:], in_=m_kj_bytes[b * P : (b + 1) * P, k0 : k0 + nk, :].rearrange("e k d -> e (k d)")
+            )
+
+        scale = keep.tile([P, D], F32, name="scale", align_bytes=64)
+        wd_raw = keep.tile([P, C], I32, name="wd_raw", align_bytes=64)
+        wd = keep.tile([P, C], I32, name="wd", align_bytes=64)
+        wds_raw = keep.tile([P, C], U8, name="wds_raw", align_bytes=64)
+        wds = keep.tile([P, C], U8, name="wds", align_bytes=64)
+        wb = keep.tile([P, 2, D], I32, name="wb", align_bytes=64)
+        wbs = keep.tile([P, D], U8, name="wbs", align_bytes=64)
+        sb = keep.tile([P, 2, K * NB], BF16, name="sb", align_bytes=64)
+        mji = keep.tile([P, 2, D], BF16, name="mji", align_bytes=64)
+        grow = keep.tile([P, NBC], BF16, name="grow", align_bytes=64)
+        ones = keep.tile([P, P], BF16, name="ones", align_bytes=64)
+        ident = keep.tile([P, P], F32, name="ident", align_bytes=64)
+        dummy = keep.tile([P, 1], F32, name="dummy", align_bytes=64)
+
+        nc.scalar.dma_start(out=scale[:], in_=m_kj_scale.rearrange("a b k -> (a b k)").partition_broadcast(P))
+        nc.gpsimd.memset(dummy[:], 0.0)
+        make_identity(nc, ident[:])
+        nc.gpsimd.memset(ones[:], 1.0)
+        nc.vector.memset(wds_raw[:].bitcast(I32), 0)
+        nc.vector.memset(wbs[:].bitcast(I32), 0)
+        nc.vector.memset(grow[:], 0.0)
+
+        load_raw(0)
+        nc.sync.dma_start(out=wd_raw[:], in_=w_down_words[0].rearrange("p n t -> p (n t)").bitcast(I32))
+        for q in range(4):
+            nc.sync.dma_start(
+                out=wds_raw[32 * q : 32 * q + 4, :].bitcast(I32), in_=w_down_scales[0, 4 * q : 4 * q + 4, :].bitcast(I32)
+            )
+        load_raw(1)
+        nc.sync.dma_start(out=grow[0:1, :], in_=gain.rearrange("(o k) -> o k", o=1))
+        nc.sync.dma_start(out=sb[:], in_=sbf.rearrange("(b e) k n -> e b (k n)", b=2))
+        load_raw(2)
+        for g in range(2):
+            nc.sync.dma_start(out=wb[:, g, :], in_=w_bil_words[g].rearrange("p n t -> p (n t)").bitcast(I32))
+        for g in range(2):
+            for q in range(4):
+                nc.sync.dma_start(
+                    out=wbs[32 * q + 4 * g : 32 * q + 4 * g + 4, :].bitcast(I32),
+                    in_=w_bil_scales[g, 4 * q : 4 * q + 4, :].bitcast(I32),
+                )
+        for ci in range(3, len(raws)):
+            load_raw(ci)
+        nc.sync.dma_start(out=mji[:], in_=m_ji.rearrange("(b e) d -> e b d", b=2))
+
+        nc.scalar.activation(out=dummy[:], in_=dummy[:], func=ACT.Silu)
+
+        gps = psum.tile([P, 2, 2, 256], BF16, name="gps")
+
+        def prepare_weights():
+            nc.vector.tensor_copy(
+                out=wd[:].rearrange("p (u q e) -> p q u e", u=2, q=32), in_=wd_raw[:].rearrange("p (q u e) -> p q u e", u=2, q=32)
+            )
+            nc.vector.tensor_copy(
+                out=wds[:].rearrange("p (u q e) -> p q u e", u=2, q=32), in_=wds_raw[:].rearrange("p (q u e) -> p q u e", u=2, q=32)
+            )
+
+        def prepare_gain():
+            for g in range(2):
+                nc.tensor.matmul(
+                    out=gps[:, g].rearrange("p u (m e) -> p u m e", e=2),
+                    lhsT=ones[:],
+                    rhs=grow[:, g * 512 : (g + 1) * 512].rearrange("p (m u e) -> p u m e", u=2, e=2),
+                    start=True,
+                    stop=True,
+                )
+
+        st = {}
+
+        def widen(s, j):
+            if j == 0:
+                mw = work.tile([P, 2, D], BF16, name="mw", bufs=3, align_bytes=64)
+                st["mw", s] = mw
+            raw, r = where[2 * s + j]
+            nc.vector.tensor_tensor(
+                out=st["mw", s][:, j, :], in0=raw[:, r * D : (r + 1) * D].bitcast(FP8), in1=scale[:], op=ALU.mult
+            )
+
+        def tr1(s):
+            ps1 = psum.tile([P, 2, 2, P], F32, name="ps1")
+            st["ps1", s] = ps1
+            words = st["mw", s][:].rearrange("p j k -> p (j k)").bitcast(F32)
+            for j in range(2):
+                for u in range(2):
+                    nc.tensor.transpose(ps1[:, j, u, :], words[:, 256 * j + u : 256 * (j + 1) : 2], ident[:])
+
+        def co1(s):
+            mg = work.tile([P, 2 * P * 4], BF16, name="mg", align_bytes=64)
+            st["mg", s] = mg
+            nc.scalar.copy(
+                out=mg[:].bitcast(F32).rearrange("p (j r u) -> p j r u", j=2, u=2),
+                in_=st["ps1", s][:].rearrange("p j u r -> p j r u"),
+            )
+
+        def quant_m(s):
+            mq = work.tile([P, 2 * P], I32, name="mq", align_bytes=64)
+            ms = work.tile([P, 2 * P], U8, name="ms", align_bytes=64)
+            st["mq", s] = (mq, ms)
+            nc.vector.quantize_mx(out=mq[:].bitcast(FP8X4), scales=ms[:], in_=st["mg", s][:])
+
+        def mx1(s):
+            ps2 = psum.tile([P, 2, C], F32, name="ps2")
+            st["ps2", s] = ps2
+            mq, ms = st["mq", s]
+            for j in range(2):
+                nc.tensor.matmul_mx(
+                    out=ps2[:, j, :],
+                    lhsT=mq[:, j * P : (j + 1) * P].bitcast(FP8X4),
+                    lhsT_scale=ms[:, j * P : (j + 1) * P],
+                    rhs=wd[:].bitcast(FP8X4),
+                    rhs_scale=wds[:],
+                    start=True,
+                    stop=True,
+                )
+
+        def silu1(s):
+            x = work.tile([P, 2, C], F32, name="x", align_bytes=64)
+            st["x", s] = x
+            nc.scalar.activation(out=x[:], in_=st["ps2", s][:], func=ACT.Silu)
+
+        def outer(s, j):
+            p2 = work.tile([P, 2, 2, 256], BF16, name="p2", bufs=4, align_bytes=64)
+            st["p2", s, j] = p2
+            x = st["x", s]
+            b, k = divmod(2 * s + j, K)
+            for n in range(NB):
+                g, h = divmod(n, 4)
+                cols = slice(64 * h, 64 * h + 64)
+                nc.vector.scalar_tensor_tensor(
+                    out=p2[:, g, :, cols],
+                    in0=x[:, j, :].rearrange("p (u c) -> p u c", u=2),
+                    scalar=sb[:, b, k * NB + n : k * NB + n + 1],
+                    in1=gps[:, g, :, cols],
+                    op0=ALU.mult,
+                    op1=ALU.mult,
+                )
+
+        def tr2(s, j):
+            ps3 = psum.tile([P, 4, P], F32, name="ps3", bufs=2)
+            st["ps3", s, j] = ps3
+            words = st["p2", s, j][:].rearrange("p g u c -> p (g u c)").bitcast(F32)
+            for v in range(4):
+                nc.tensor.transpose(ps3[:, v, :], words[:, P * v : P * (v + 1)], ident[:])
+
+        def co2(s, j):
+            if j == 0:
+                pg = work.tile([P, 2 * 2 * P * 4], BF16, name="pg", align_bytes=64)
+                st["pg", s] = pg
+            w = st["pg", s][:].bitcast(F32).rearrange("p (g r u) -> p g r u", g=2, u=2)
+            nc.scalar.copy(
+                out=w[:, :, j * P : (j + 1) * P, :], in_=st["ps3", s, j][:].rearrange("p (g u) r -> p g r u", g=2)
+            )
+
+        def quant_p(s):
+            pq = work.tile([P, 2, 2 * P], I32, name="pq", align_bytes=64)
+            pss = work.tile([P, 2, 2 * P], U8, name="pss", align_bytes=64)
+            st["pq", s] = (pq, pss)
+            nc.vector.quantize_mx(
+                out=pq[:].rearrange("p g r -> p (g r)").bitcast(FP8X4),
+                scales=pss[:].rearrange("p g r -> p (g r)"),
+                in_=st["pg", s][:],
+            )
+
+        def mx2(s, half):
+            ps4 = psum.tile([P, 2, 2 * P], F32, name="ps4", bufs=2)
+            st["ps4", s, half] = ps4
+            pq, pss = st["pq", s]
+            for h in range(2):
+                d0 = (2 * half + h) * P
+                for g in range(2):
+                    nc.tensor.matmul_mx(
+                        out=ps4[:, h, :],
+                        lhsT=wb[:, g, d0 : d0 + P].bitcast(FP8X4),
+                        lhsT_scale=wbs[4 * g : P, d0 : d0 + P],
+                        rhs=pq[:, g, :].bitcast(FP8X4),
+                        rhs_scale=pss[:, g, :],
+                        start=(g == 0),
+                        stop=(g == 1),
+                    )
+
+        def silu2(s, half):
+            t = work.tile([P, 2, 2 * P], F32, name="t", bufs=4, align_bytes=64)
+            st["t", s, half] = t
+            nc.scalar.activation(out=t[:], in_=st["ps4", s, half][:], func=ACT.Silu)
+
+        def accumulate(s, half):
+            b, k = divmod(s, PPB)
+            if k == 0 and half == 0:
+                acc = psum.tile([P, D], F32, name="acc")
+                st["acc", b] = acc
+            acc = st["acc", b]
+            t = st["t", s, half]
+            for h in range(2):
+                d0 = (2 * half + h) * P
+                for j in range(2):
+                    nc.tensor.matmul(
+                        out=acc[:, d0 : d0 + P],
+                        lhsT=t[:, h, j * P : (j + 1) * P],
+                        rhs=ident[:],
+                        is_transpose=True,
+                        start=(k == 0 and half == 0 and h == 0 and j == 0),
+                        stop=(k == PPB - 1 and half == 1 and h == 1 and j == 1),
+                    )
+
+        def finish(b):
+            o = work.tile([P, D], F32, name="o", bufs=2, align_bytes=64)
+            nc.vector.scalar_tensor_tensor(
+                out=o[:], in0=st["acc", b][:], scalar=0.25, in1=mji[:, b, :], op0=ALU.mult, op1=ALU.add
+            )
+            nc.sync.dma_start(out=out[b * P : (b + 1) * P, :], in_=o[:])
+
+        def ok(s):
+            return 0 <= s < PAIRS
+
+        for s in range(-3, PAIRS + 2):
+            def pe_head():
+                if ok(s - 1):
+                    tr2(s - 1, 1)
+                if ok(s + 2):
+                    tr1(s + 2)
+                if ok(s + 1):
+                    mx1(s + 1)
+
+            def sc_head():
+                if ok(s - 1):
+                    co2(s - 1, 1)
+                if ok(s + 2):
+                    co1(s + 2)
+                if ok(s + 1):
+                    silu1(s + 1)
+
+            pe_head()
+            sc_head()
+            if ok(s):
+                outer(s, 0)
+                tr2(s, 0)
+                co2(s, 0)
+            if ok(s + 3):
+                widen(s + 3, 0)
+            if ok(s - 1):
+                quant_p(s - 1)
+            if ok(s - 2):
+                accumulate(s - 2, 0)
+                accumulate(s - 2, 1)
+                if (s - 2) % PPB == PPB - 1:
+                    finish((s - 2) // PPB)
+            if ok(s - 1):
+                for half in range(2):
+                    mx2(s - 1, half)
+                    silu2(s - 1, half)
+            if ok(s + 3):
+                widen(s + 3, 1)
+            if ok(s):
+                outer(s, 1)
+            if s == -3:
+                prepare_weights()
+            if s == -2:
+                prepare_gain()
+            if ok(s + 2):
+                quant_m(s + 2)

@@ -18,6 +18,8 @@ NBC = NB * C
 FLOPS = 2 * E * K * D * C + 2 * E * K * NBC * D
 PAIRS = E * K // P // 2
 PPB = K // 2
+SHARED = tuple(range(NB - 2, NB))
+OWN = tuple(n for n in range(NB) if n not in SHARED)
 
 
 def tile_dimenettripletbilinear_w8_kernel(
@@ -60,6 +62,8 @@ def tile_dimenettripletbilinear_w8_kernel(
         grow = keep.tile([P, NBC], BF16, name="grow", align_bytes=64)
         ones = keep.tile([P, P], BF16, name="ones", align_bytes=64)
         ident = keep.tile([P, P], F32, name="ident", align_bytes=64)
+        sb32 = keep.tile([P, 2, K * NB], F32, name="sb32", align_bytes=64)
+        gsh = keep.tile([P, len(SHARED), C], BF16, name="gsh", align_bytes=64)
         dummy = keep.tile([P, 1], F32, name="dummy", align_bytes=64)
 
         nc.scalar.dma_start(out=scale[:], in_=m_kj_scale.rearrange("a b k -> (a b k)").partition_broadcast(P))
@@ -112,6 +116,37 @@ def tile_dimenettripletbilinear_w8_kernel(
                     rhs=grow[:, g * 512 : (g + 1) * 512].rearrange("p (m u e) -> p u m e", u=2, e=2),
                     start=True,
                     stop=True,
+                )
+
+        def prepare_shared():
+            nc.vector.tensor_copy(out=sb32[:], in_=sb[:])
+            for i, n in enumerate(SHARED):
+                g, h = divmod(n, 4)
+                nc.vector.tensor_copy(
+                    out=gsh[:, i, :].rearrange("p (u c) -> p u c", u=2), in_=gps[:, g, :, 64 * h : 64 * h + 64]
+                )
+
+        def pool_share(s):
+            xg = work.tile([P, 2, len(SHARED), C], F32, name="xg", align_bytes=64)
+            st["xg", s] = xg
+            nc.gpsimd.tensor_tensor(
+                out=xg[:],
+                in0=st["x", s][:].unsqueeze(2).to_broadcast([P, 2, len(SHARED), C]),
+                in1=gsh[:].unsqueeze(1).to_broadcast([P, 2, len(SHARED), C]),
+                op=ALU.mult,
+            )
+
+        def scalar_share(s, j):
+            p2 = work.tile([P, 2, 2, 256], BF16, name="p2", bufs=6, align_bytes=64)
+            st["p2", s, j] = p2
+            b, k = divmod(2 * s + j, K)
+            for i, n in enumerate(SHARED):
+                g, h = divmod(n, 4)
+                nc.scalar.activation(
+                    out=p2[:, g, :, 64 * h : 64 * h + 64],
+                    in_=st["xg", s][:, j, i, :].rearrange("p (u c) -> p u c", u=2),
+                    func=ACT.Copy,
+                    scale=sb32[:, b, k * NB + n : k * NB + n + 1],
                 )
 
         st = {}
@@ -168,11 +203,10 @@ def tile_dimenettripletbilinear_w8_kernel(
             nc.scalar.activation(out=x[:], in_=st["ps2", s][:], func=ACT.Silu)
 
         def outer(s, j):
-            p2 = work.tile([P, 2, 2, 256], BF16, name="p2", bufs=4, align_bytes=64)
-            st["p2", s, j] = p2
+            p2 = st["p2", s, j]
             x = st["x", s]
             b, k = divmod(2 * s + j, K)
-            for n in range(NB):
+            for n in OWN:
                 g, h = divmod(n, 4)
                 cols = slice(64 * h, 64 * h + 64)
                 nc.vector.scalar_tensor_tensor(
@@ -261,49 +295,29 @@ def tile_dimenettripletbilinear_w8_kernel(
         def ok(s):
             return 0 <= s < PAIRS
 
-        for s in range(-3, PAIRS + 2):
-            def pe_head():
-                if ok(s - 1):
-                    tr2(s - 1, 1)
-                if ok(s + 2):
-                    tr1(s + 2)
-                if ok(s + 1):
-                    mx1(s + 1)
-
-            def sc_head():
-                if ok(s - 1):
-                    co2(s - 1, 1)
-                if ok(s + 2):
-                    co1(s + 2)
-                if ok(s + 1):
-                    silu1(s + 1)
-
-            pe_head()
-            sc_head()
-            if ok(s):
-                outer(s, 0)
-                tr2(s, 0)
-                co2(s, 0)
-            if ok(s + 3):
-                widen(s + 3, 0)
-            if ok(s - 1):
-                quant_p(s - 1)
-            if ok(s - 2):
-                accumulate(s - 2, 0)
-                accumulate(s - 2, 1)
-                if (s - 2) % PPB == PPB - 1:
-                    finish((s - 2) // PPB)
-            if ok(s - 1):
-                for half in range(2):
-                    mx2(s - 1, half)
-                    silu2(s - 1, half)
-            if ok(s + 3):
-                widen(s + 3, 1)
-            if ok(s):
-                outer(s, 1)
-            if s == -3:
+        def pair_stage(kind, s, j):
+            if kind == "mx1" and s == 0:
                 prepare_weights()
-            if s == -2:
+            if kind == "silu1" and s == 0:
                 prepare_gain()
-            if ok(s + 2):
-                quant_m(s + 2)
+                prepare_shared()
+            if kind == "acc" and s == PPB and j == 0:
+                finish(0)
+            fn = stages[kind]
+            if j is None:
+                fn(s)
+            else:
+                fn(s, j)
+            if kind == "acc" and s == PAIRS - 1 and j == 1:
+                finish(1)
+
+        stages = {
+            "widen": widen, "tr1": tr1, "co1": co1, "quant_m": quant_m, "mx1": mx1, "silu1": silu1,
+            "pool": pool_share, "sshare": scalar_share, "outer": outer, "tr2": tr2, "co2": co2,
+            "quant_p": quant_p, "mx2": mx2, "silu2": silu2, "acc": accumulate,
+        }
+        order = [('outer', 0, 0), ('outer', 0, 1), ('co2', -1, 0), ('silu2', -3, 1), ('widen', 5, 0), ('mx2', -2, 1), ('quant_m', 3, None), ('silu1', 2, None), ('sshare', 1, 1), ('co2', -1, 1), ('pool', 2, None), ('tr1', 4, None), ('tr2', 0, 0), ('acc', -3, 1), ('sshare', 1, 0), ('mx1', 3, None), ('tr2', 0, 1), ('quant_p', -1, None), ('widen', 5, 1), ('silu2', -2, 0), ('mx2', -1, 0), ('co1', 4, None), ('acc', -2, 0)]
+        for s in range(-8, PAIRS + 6):
+            for kind, off, j in order:
+                if 0 <= s + off < PAIRS:
+                    pair_stage(kind, s + off, j)

@@ -16,10 +16,18 @@ P = 128
 E, K, D, C, NB = 256, 16, 512, 128, 8
 NBC = NB * C
 FLOPS = 2 * E * K * D * C + 2 * E * K * NBC * D
-PAIRS = E * K // P // 2
-PPB = K // 2
-SHARED = tuple(range(NB - 2, NB))
-OWN = tuple(n for n in range(NB) if n not in SHARED)
+
+PAIRS = E * K // (2 * P)
+PAIRS_PER_BLOCK = K // 2
+MAX_SHARE = 3
+PREFETCH = 5
+CHUNKS = (2, 2, 4, 4, 4, 4, 4, 4, 4)
+
+
+def share(s):
+    if s >= PAIRS - 3:
+        return 1
+    return 3 if s % 3 == 0 else 2
 
 
 def tile_dimenettripletbilinear_w8_kernel(
@@ -32,292 +40,296 @@ def tile_dimenettripletbilinear_w8_kernel(
         psum = ctx.enter_context(tc.psum_pool(name="psum", bufs=1))
         ctx.enter_context(tc.manual_schedule())
 
-        chunk_k = [2, 2, 4, 4, 4, 4, 4, 4, 4]
-        raws = []
-        where = {}
-        pos = 0
-        for ci, nk in enumerate(chunk_k):
-            raw = keep.tile([P, nk * D], U8, name="raw%d" % ci, align_bytes=64)
-            raws.append((raw, pos, nk))
-            for j in range(nk):
-                where[pos + j] = (raw, j)
-            pos += nk
-
-        def load_raw(ci):
-            raw, p0, nk = raws[ci]
-            b, k0 = divmod(p0, K)
-            nc.sync.dma_start(
-                out=raw[:], in_=m_kj_bytes[b * P : (b + 1) * P, k0 : k0 + nk, :].rearrange("e k d -> e (k d)")
-            )
-
+        scale_cols = keep.tile([P, 4], F32, name="scale_cols", align_bytes=64)
         scale = keep.tile([P, D], F32, name="scale", align_bytes=64)
-        wd_raw = keep.tile([P, C], I32, name="wd_raw", align_bytes=64)
-        wd = keep.tile([P, C], I32, name="wd", align_bytes=64)
-        wds_raw = keep.tile([P, C], U8, name="wds_raw", align_bytes=64)
-        wds = keep.tile([P, C], U8, name="wds", align_bytes=64)
-        wb = keep.tile([P, 2, D], I32, name="wb", align_bytes=64)
-        wbs = keep.tile([P, D], U8, name="wbs", align_bytes=64)
-        sb = keep.tile([P, 2, K * NB], BF16, name="sb", align_bytes=64)
-        mji = keep.tile([P, 2, D], BF16, name="mji", align_bytes=64)
-        grow = keep.tile([P, NBC], BF16, name="grow", align_bytes=64)
+        down_raw = keep.tile([P, C], I32, name="down_raw", align_bytes=64)
+        down_scales_raw = keep.tile([P, C], U8, name="down_scales_raw", align_bytes=64)
+        down = keep.tile([P, C], I32, name="down", align_bytes=64)
+        down_scales = keep.tile([P, C], U8, name="down_scales", align_bytes=64)
+        bil = keep.tile([P, 2, D], I32, name="bil", align_bytes=64)
+        bil_scales = keep.tile([P, D], U8, name="bil_scales", align_bytes=64)
+        basis = keep.tile([P, 2, K * NB], BF16, name="basis", align_bytes=64)
+        basis_f32 = keep.tile([P, 2, K * NB], F32, name="basis_f32", align_bytes=64)
+        residual = keep.tile([P, 2, D], BF16, name="residual", align_bytes=64)
+        gain_row = keep.tile([P, NBC], BF16, name="gain_row", align_bytes=64)
+        gain_shared = keep.tile([P, MAX_SHARE, C], BF16, name="gain_shared", align_bytes=64)
         ones = keep.tile([P, P], BF16, name="ones", align_bytes=64)
         ident = keep.tile([P, P], F32, name="ident", align_bytes=64)
-        sb32 = keep.tile([P, 2, K * NB], F32, name="sb32", align_bytes=64)
-        gsh = keep.tile([P, len(SHARED), C], BF16, name="gsh", align_bytes=64)
-        dummy = keep.tile([P, 1], F32, name="dummy", align_bytes=64)
+        first_silu = keep.tile([P, 1], F32, name="first_silu", align_bytes=64)
+        gain_all = psum.tile([P, 2, 2, 256], BF16, name="gain_all")
 
-        nc.scalar.dma_start(out=scale[:], in_=m_kj_scale.rearrange("a b k -> (a b k)").partition_broadcast(P))
-        nc.gpsimd.memset(dummy[:], 0.0)
+        nc.gpsimd.memset(first_silu[:], 0.0)
         make_identity(nc, ident[:])
         nc.gpsimd.memset(ones[:], 1.0)
-        nc.vector.memset(wds_raw[:].bitcast(I32), 0)
-        nc.vector.memset(wbs[:].bitcast(I32), 0)
-        nc.vector.memset(grow[:], 0.0)
+        nc.vector.memset(down_scales_raw[:].bitcast(I32), 0)
+        nc.vector.memset(bil_scales[:].bitcast(I32), 0)
+        nc.vector.memset(gain_row[:], 0.0)
 
-        load_raw(0)
-        nc.sync.dma_start(out=wd_raw[:], in_=w_down_words[0].rearrange("p n t -> p (n t)").bitcast(I32))
-        for q in range(4):
+        byte_rows = []
+
+        def load_bytes(k_count):
+            b, k0 = divmod(len(byte_rows), K)
+            chunk = keep.tile([P, k_count * D], U8, name="bytes_%d_%d" % (b, k0), align_bytes=64)
             nc.sync.dma_start(
-                out=wds_raw[32 * q : 32 * q + 4, :].bitcast(I32), in_=w_down_scales[0, 4 * q : 4 * q + 4, :].bitcast(I32)
+                out=chunk[:], in_=m_kj_bytes[b * P : (b + 1) * P, k0 : k0 + k_count, :].rearrange("e k d -> e (k d)")
             )
-        load_raw(1)
-        nc.sync.dma_start(out=grow[0:1, :], in_=gain.rearrange("(o k) -> o k", o=1))
-        nc.sync.dma_start(out=sb[:], in_=sbf.rearrange("(b e) k n -> e b (k n)", b=2))
-        load_raw(2)
+            byte_rows.extend([chunk[:, j * D : (j + 1) * D] for j in range(k_count)])
+
+        nc.sync.dma_start(out=scale_cols[:], in_=m_kj_scale.rearrange("a b (p t) -> p (a b t)", t=4))
+        load_bytes(CHUNKS[0])
+        for quad in range(4):
+            nc.sync.dma_start(
+                out=down_scales_raw[32 * quad : 32 * quad + 4, :].bitcast(I32),
+                in_=w_down_scales[0, 4 * quad : 4 * quad + 4, :].bitcast(I32),
+            )
+        nc.sync.dma_start(out=down_raw[:], in_=w_down_words[0].rearrange("p n t -> p (n t)").bitcast(I32))
+        for k_count in CHUNKS[1:]:
+            load_bytes(k_count)
         for g in range(2):
-            nc.sync.dma_start(out=wb[:, g, :], in_=w_bil_words[g].rearrange("p n t -> p (n t)").bitcast(I32))
-        for g in range(2):
-            for q in range(4):
-                nc.sync.dma_start(
-                    out=wbs[32 * q + 4 * g : 32 * q + 4 * g + 4, :].bitcast(I32),
-                    in_=w_bil_scales[g, 4 * q : 4 * q + 4, :].bitcast(I32),
-                )
-        for ci in range(3, len(raws)):
-            load_raw(ci)
-        nc.sync.dma_start(out=mji[:], in_=m_ji.rearrange("(b e) d -> e b d", b=2))
-
-        nc.scalar.activation(out=dummy[:], in_=dummy[:], func=ACT.Silu)
-
-        gps = psum.tile([P, 2, 2, 256], BF16, name="gps")
-
-        def prepare_weights():
-            nc.vector.tensor_copy(
-                out=wd[:].rearrange("p (u q e) -> p q u e", u=2, q=32), in_=wd_raw[:].rearrange("p (q u e) -> p q u e", u=2, q=32)
+            nc.sync.dma_start(out=bil[:, g, :], in_=w_bil_words[g].rearrange("p n t -> p (n t)").bitcast(I32))
+        for quad in range(4):
+            nc.sync.dma_start(
+                out=bil_scales[32 * quad : 32 * quad + 8, :].bitcast(I32),
+                in_=w_bil_scales[:, 4 * quad : 4 * quad + 4, :].bitcast(I32),
             )
-            nc.vector.tensor_copy(
-                out=wds[:].rearrange("p (u q e) -> p q u e", u=2, q=32), in_=wds_raw[:].rearrange("p (q u e) -> p q u e", u=2, q=32)
-            )
+        nc.scalar.dma_start(out=gain_row[0:1, :], in_=gain.rearrange("(o k) -> o k", o=1))
+        nc.scalar.dma_start(out=basis[:], in_=sbf.rearrange("(b e) k n -> e b (k n)", b=2))
+        nc.scalar.dma_start(out=residual[:], in_=m_ji.rearrange("(b e) d -> e b d", b=2))
 
-        def prepare_gain():
+        nc.scalar.activation(out=first_silu[:], in_=first_silu[:], func=ACT.Silu)
+
+        spread = psum.tile([P, 4, P], F32, name="words2", bufs=2)
+        for t in range(4):
+            nc.tensor.transpose(spread[:, t, :], scale_cols[:, t : t + 1].to_broadcast([P, P]), ident[:])
+        nc.vector.tensor_copy(out=scale[:].rearrange("p (k t) -> p k t", t=4), in_=spread[:].rearrange("p t k -> p k t"))
+
+        def fill_gain():
             for g in range(2):
                 nc.tensor.matmul(
-                    out=gps[:, g].rearrange("p u (m e) -> p u m e", e=2),
+                    out=gain_all[:, g].rearrange("p u (m e) -> p u m e", e=2),
                     lhsT=ones[:],
-                    rhs=grow[:, g * 512 : (g + 1) * 512].rearrange("p (m u e) -> p u m e", u=2, e=2),
+                    rhs=gain_row[:, g * 512 : (g + 1) * 512].rearrange("p (m u e) -> p u m e", u=2, e=2),
                     start=True,
                     stop=True,
                 )
 
-        def prepare_shared():
-            nc.vector.tensor_copy(out=sb32[:], in_=sb[:])
-            for i, n in enumerate(SHARED):
-                g, h = divmod(n, 4)
+        def prepare_sharing():
+            nc.vector.tensor_copy(out=basis_f32[:], in_=basis[:])
+            for i in range(MAX_SHARE):
+                g, h = divmod(NB - MAX_SHARE + i, 4)
                 nc.vector.tensor_copy(
-                    out=gsh[:, i, :].rearrange("p (u c) -> p u c", u=2), in_=gps[:, g, :, 64 * h : 64 * h + 64]
+                    out=gain_shared[:, i, :].rearrange("p (u c) -> p u c", u=2),
+                    in_=gain_all[:, g, :, 64 * h : 64 * h + 64],
                 )
 
-        def pool_share(s):
-            xg = work.tile([P, 2, len(SHARED), C], F32, name="xg", align_bytes=64)
-            st["xg", s] = xg
-            nc.gpsimd.tensor_tensor(
-                out=xg[:],
-                in0=st["x", s][:].unsqueeze(2).to_broadcast([P, 2, len(SHARED), C]),
-                in1=gsh[:].unsqueeze(1).to_broadcast([P, 2, len(SHARED), C]),
-                op=ALU.mult,
-            )
-
-        def scalar_share(s, j):
-            p2 = work.tile([P, 2, 2, 256], BF16, name="p2", bufs=6, align_bytes=64)
-            st["p2", s, j] = p2
-            b, k = divmod(2 * s + j, K)
-            for i, n in enumerate(SHARED):
-                g, h = divmod(n, 4)
-                nc.scalar.activation(
-                    out=p2[:, g, :, 64 * h : 64 * h + 64],
-                    in_=st["xg", s][:, j, i, :].rearrange("p (u c) -> p u c", u=2),
-                    func=ACT.Copy,
-                    scale=sb32[:, b, k * NB + n : k * NB + n + 1],
+        def permute_w_down():
+            for dst, src in ((down, down_raw), (down_scales, down_scales_raw)):
+                nc.vector.tensor_copy(
+                    out=dst[:].rearrange("p (u q e) -> p q u e", u=2, q=32),
+                    in_=src[:].rearrange("p (q u e) -> p q u e", u=2, q=32),
                 )
 
-        st = {}
+        tiles = {}
 
         def widen(s, j):
             if j == 0:
-                mw = work.tile([P, 2, D], BF16, name="mw", bufs=3, align_bytes=64)
-                st["mw", s] = mw
-            raw, r = where[2 * s + j]
+                tiles["m", s] = work.tile([P, 2, D], BF16, name="m", align_bytes=64)
             nc.vector.tensor_tensor(
-                out=st["mw", s][:, j, :], in0=raw[:, r * D : (r + 1) * D].bitcast(FP8), in1=scale[:], op=ALU.mult
+                out=tiles["m", s][:, j, :], in0=byte_rows[2 * s + j].bitcast(FP8), in1=scale[:], op=ALU.mult
             )
 
-        def tr1(s):
-            ps1 = psum.tile([P, 2, 2, P], F32, name="ps1")
-            st["ps1", s] = ps1
-            words = st["mw", s][:].rearrange("p j k -> p (j k)").bitcast(F32)
+        def turn_m(s):
+            words1 = psum.tile([P, 2, 2, P], F32, name="words1")
+            tiles["words1", s] = words1
+            words = tiles["m", s][:].rearrange("p j k -> p (j k)").bitcast(F32)
             for j in range(2):
                 for u in range(2):
-                    nc.tensor.transpose(ps1[:, j, u, :], words[:, 256 * j + u : 256 * (j + 1) : 2], ident[:])
+                    nc.tensor.transpose(words1[:, j, u, :], words[:, 256 * j + u : 256 * (j + 1) : 2], ident[:])
 
-        def co1(s):
-            mg = work.tile([P, 2 * P * 4], BF16, name="mg", align_bytes=64)
-            st["mg", s] = mg
+        def copy_m(s):
+            m_t = work.tile([P, 2 * P * 4], BF16, name="m_t", align_bytes=64)
+            tiles["m_t", s] = m_t
             nc.scalar.copy(
-                out=mg[:].bitcast(F32).rearrange("p (j r u) -> p j r u", j=2, u=2),
-                in_=st["ps1", s][:].rearrange("p j u r -> p j r u"),
+                out=m_t[:].bitcast(F32).rearrange("p (j r u) -> p j r u", j=2, u=2),
+                in_=tiles["words1", s][:].rearrange("p j u r -> p j r u"),
             )
 
-        def quant_m(s):
-            mq = work.tile([P, 2 * P], I32, name="mq", align_bytes=64)
-            ms = work.tile([P, 2 * P], U8, name="ms", align_bytes=64)
-            st["mq", s] = (mq, ms)
-            nc.vector.quantize_mx(out=mq[:].bitcast(FP8X4), scales=ms[:], in_=st["mg", s][:])
+        def quantise_m(s):
+            codes = work.tile([P, 2 * P], I32, name="m_codes", align_bytes=64)
+            scales = work.tile([P, 2 * P], U8, name="m_scales", align_bytes=64)
+            tiles["mq", s] = (codes, scales)
+            nc.vector.quantize_mx(out=codes[:].bitcast(FP8X4), scales=scales[:], in_=tiles["m_t", s][:])
 
-        def mx1(s):
-            ps2 = psum.tile([P, 2, C], F32, name="ps2")
-            st["ps2", s] = ps2
-            mq, ms = st["mq", s]
+        def multiply_down(s):
+            y = psum.tile([P, 2, C], F32, name="y")
+            tiles["y", s] = y
+            codes, scales = tiles["mq", s]
             for j in range(2):
+                rows = slice(j * P, (j + 1) * P)
                 nc.tensor.matmul_mx(
-                    out=ps2[:, j, :],
-                    lhsT=mq[:, j * P : (j + 1) * P].bitcast(FP8X4),
-                    lhsT_scale=ms[:, j * P : (j + 1) * P],
-                    rhs=wd[:].bitcast(FP8X4),
-                    rhs_scale=wds[:],
+                    out=y[:, j, :],
+                    lhsT=codes[:, rows].bitcast(FP8X4),
+                    lhsT_scale=scales[:, rows],
+                    rhs=down[:].bitcast(FP8X4),
+                    rhs_scale=down_scales[:],
                     start=True,
                     stop=True,
                 )
 
-        def silu1(s):
+        def silu_x(s):
             x = work.tile([P, 2, C], F32, name="x", align_bytes=64)
-            st["x", s] = x
-            nc.scalar.activation(out=x[:], in_=st["ps2", s][:], func=ACT.Silu)
+            tiles["x", s] = x
+            nc.scalar.activation(out=x[:], in_=tiles["y", s][:], func=ACT.Silu)
+
+        def gain_product(s):
+            xg = work.tile([P, 2, MAX_SHARE, C], F32, name="xg", align_bytes=64)
+            tiles["xg", s] = xg
+            m = share(s)
+            nc.gpsimd.tensor_tensor(
+                out=xg[:, :, MAX_SHARE - m :, :],
+                in0=tiles["x", s][:].unsqueeze(2).to_broadcast([P, 2, m, C]),
+                in1=gain_shared[:, MAX_SHARE - m :, :].unsqueeze(1).to_broadcast([P, 2, m, C]),
+                op=ALU.mult,
+            )
+
+        def basis_product(s, j):
+            prod = work.tile([P, 2, 2, 256], BF16, name="prod", bufs=6, align_bytes=64)
+            tiles["prod", s, j] = prod
+            b, k = divmod(2 * s + j, K)
+            for n in range(NB - share(s), NB):
+                g, h = divmod(n, 4)
+                nc.scalar.activation(
+                    out=prod[:, g, :, 64 * h : 64 * h + 64],
+                    in_=tiles["xg", s][:, j, n - NB + MAX_SHARE, :].rearrange("p (u c) -> p u c", u=2),
+                    func=ACT.Copy,
+                    scale=basis_f32[:, b, k * NB + n : k * NB + n + 1],
+                )
 
         def outer(s, j):
-            p2 = st["p2", s, j]
-            x = st["x", s]
+            prod = tiles["prod", s, j]
             b, k = divmod(2 * s + j, K)
-            for n in OWN:
+            for n in range(NB - share(s)):
                 g, h = divmod(n, 4)
                 cols = slice(64 * h, 64 * h + 64)
                 nc.vector.scalar_tensor_tensor(
-                    out=p2[:, g, :, cols],
-                    in0=x[:, j, :].rearrange("p (u c) -> p u c", u=2),
-                    scalar=sb[:, b, k * NB + n : k * NB + n + 1],
-                    in1=gps[:, g, :, cols],
+                    out=prod[:, g, :, cols],
+                    in0=tiles["x", s][:, j, :].rearrange("p (u c) -> p u c", u=2),
+                    scalar=basis[:, b, k * NB + n : k * NB + n + 1],
+                    in1=gain_all[:, g, :, cols],
                     op0=ALU.mult,
                     op1=ALU.mult,
                 )
 
-        def tr2(s, j):
-            ps3 = psum.tile([P, 4, P], F32, name="ps3", bufs=2)
-            st["ps3", s, j] = ps3
-            words = st["p2", s, j][:].rearrange("p g u c -> p (g u c)").bitcast(F32)
-            for v in range(4):
-                nc.tensor.transpose(ps3[:, v, :], words[:, P * v : P * (v + 1)], ident[:])
+        def turn_p(s, j):
+            words2 = psum.tile([P, 4, P], F32, name="words2", bufs=2)
+            tiles["words2", s, j] = words2
+            words = tiles["prod", s, j][:].rearrange("p g u c -> p (g u c)").bitcast(F32)
+            for gu in range(4):
+                nc.tensor.transpose(words2[:, gu, :], words[:, P * gu : P * (gu + 1)], ident[:])
 
-        def co2(s, j):
+        def copy_p(s, j):
             if j == 0:
-                pg = work.tile([P, 2 * 2 * P * 4], BF16, name="pg", align_bytes=64)
-                st["pg", s] = pg
-            w = st["pg", s][:].bitcast(F32).rearrange("p (g r u) -> p g r u", g=2, u=2)
+                tiles["p_t", s] = work.tile([P, 2 * 2 * P * 4], BF16, name="p_t", align_bytes=64)
+            words = tiles["p_t", s][:].bitcast(F32).rearrange("p (g r u) -> p g r u", g=2, u=2)
             nc.scalar.copy(
-                out=w[:, :, j * P : (j + 1) * P, :], in_=st["ps3", s, j][:].rearrange("p (g u) r -> p g r u", g=2)
+                out=words[:, :, j * P : (j + 1) * P, :],
+                in_=tiles["words2", s, j][:].rearrange("p (g u) r -> p g r u", g=2),
             )
 
-        def quant_p(s):
-            pq = work.tile([P, 2, 2 * P], I32, name="pq", align_bytes=64)
-            pss = work.tile([P, 2, 2 * P], U8, name="pss", align_bytes=64)
-            st["pq", s] = (pq, pss)
-            nc.vector.quantize_mx(
-                out=pq[:].rearrange("p g r -> p (g r)").bitcast(FP8X4),
-                scales=pss[:].rearrange("p g r -> p (g r)"),
-                in_=st["pg", s][:],
-            )
+        def quantise_p(s):
+            codes = work.tile([P, 2 * 2 * P], I32, name="p_codes", align_bytes=64)
+            scales = work.tile([P, 2 * 2 * P], U8, name="p_scales", align_bytes=64)
+            tiles["pq", s] = (codes, scales)
+            nc.vector.quantize_mx(out=codes[:].bitcast(FP8X4), scales=scales[:], in_=tiles["p_t", s][:])
 
-        def mx2(s, half):
-            ps4 = psum.tile([P, 2, 2 * P], F32, name="ps4", bufs=2)
-            st["ps4", s, half] = ps4
-            pq, pss = st["pq", s]
-            for h in range(2):
-                d0 = (2 * half + h) * P
+        def multiply_bil(s, half):
+            z = psum.tile([P, 2, 2 * P], F32, name="z", bufs=2)
+            tiles["z", s, half] = z
+            codes, scales = tiles["pq", s]
+            for i in range(2):
+                d_cols = slice((2 * half + i) * P, (2 * half + i + 1) * P)
                 for g in range(2):
+                    rows = slice(2 * P * g, 2 * P * (g + 1))
                     nc.tensor.matmul_mx(
-                        out=ps4[:, h, :],
-                        lhsT=wb[:, g, d0 : d0 + P].bitcast(FP8X4),
-                        lhsT_scale=wbs[4 * g : P, d0 : d0 + P],
-                        rhs=pq[:, g, :].bitcast(FP8X4),
-                        rhs_scale=pss[:, g, :],
+                        out=z[:, i, :],
+                        lhsT=bil[:, g, d_cols].bitcast(FP8X4),
+                        lhsT_scale=bil_scales[4 * g : P, d_cols],
+                        rhs=codes[:, rows].bitcast(FP8X4),
+                        rhs_scale=scales[:, rows],
                         start=(g == 0),
                         stop=(g == 1),
                     )
 
-        def silu2(s, half):
+        def silu_t(s, half):
             t = work.tile([P, 2, 2 * P], F32, name="t", bufs=4, align_bytes=64)
-            st["t", s, half] = t
-            nc.scalar.activation(out=t[:], in_=st["ps4", s, half][:], func=ACT.Silu)
+            tiles["t", s, half] = t
+            nc.scalar.activation(out=t[:], in_=tiles["z", s, half][:], func=ACT.Silu)
 
-        def accumulate(s, half):
-            b, k = divmod(s, PPB)
-            if k == 0 and half == 0:
-                acc = psum.tile([P, D], F32, name="acc")
-                st["acc", b] = acc
-            acc = st["acc", b]
-            t = st["t", s, half]
-            for h in range(2):
-                d0 = (2 * half + h) * P
+        def add_up(s, half):
+            b, pair = divmod(s, PAIRS_PER_BLOCK)
+            first, last = pair == 0 and half == 0, pair == PAIRS_PER_BLOCK - 1 and half == 1
+            if first:
+                tiles["sum", b] = psum.tile([P, D], F32, name="sum")
+            for i in range(2):
+                d0 = (2 * half + i) * P
                 for j in range(2):
                     nc.tensor.matmul(
-                        out=acc[:, d0 : d0 + P],
-                        lhsT=t[:, h, j * P : (j + 1) * P],
+                        out=tiles["sum", b][:, d0 : d0 + P],
+                        lhsT=tiles["t", s, half][:, i, j * P : (j + 1) * P],
                         rhs=ident[:],
                         is_transpose=True,
-                        start=(k == 0 and half == 0 and h == 0 and j == 0),
-                        stop=(k == PPB - 1 and half == 1 and h == 1 and j == 1),
+                        start=(first and i == 0 and j == 0),
+                        stop=(last and i == 1 and j == 1),
                     )
 
         def finish(b):
-            o = work.tile([P, D], F32, name="o", bufs=2, align_bytes=64)
-            nc.vector.scalar_tensor_tensor(
-                out=o[:], in0=st["acc", b][:], scalar=0.25, in1=mji[:, b, :], op0=ALU.mult, op1=ALU.add
-            )
-            nc.sync.dma_start(out=out[b * P : (b + 1) * P, :], in_=o[:])
+            for half in range(2):
+                cols = slice(256 * half, 256 * (half + 1))
+                o = work.tile([P, 256], F32, name="o", bufs=4, align_bytes=64)
+                nc.vector.scalar_tensor_tensor(
+                    out=o[:],
+                    in0=tiles["sum", b][:, cols],
+                    scalar=0.25,
+                    in1=residual[:, b, cols],
+                    op0=ALU.mult,
+                    op1=ALU.add,
+                )
+                nc.sync.dma_start(out=out[b * P : (b + 1) * P, cols], in_=o[:])
 
-        def ok(s):
-            return 0 <= s < PAIRS
+        def run(stage, s, *part):
+            if 0 <= s < PAIRS:
+                stage(s, *part)
 
-        def pair_stage(kind, s, j):
-            if kind == "mx1" and s == 0:
-                prepare_weights()
-            if kind == "silu1" and s == 0:
-                prepare_gain()
-                prepare_shared()
-            if kind == "acc" and s == PPB and j == 0:
+        for s in range(-PREFETCH, PAIRS + 3):
+            run(widen, s + PREFETCH, 0)
+            run(widen, s + PREFETCH, 1)
+            if s == -2:
+                prepare_sharing()
+            run(copy_p, s - 1, 1)
+            run(silu_x, s + 2)
+            run(gain_product, s + 2)
+            run(basis_product, s + 1, 0)
+            run(outer, s, 0)
+            run(outer, s, 1)
+            run(multiply_bil, s - 2, 1)
+            run(silu_t, s - 2, 0)
+            run(silu_t, s - 2, 1)
+            if s == -3:
+                fill_gain()
+            run(turn_m, s + 4)
+            run(turn_p, s, 0)
+            if s - 3 == PAIRS_PER_BLOCK:
                 finish(0)
-            fn = stages[kind]
-            if j is None:
-                fn(s)
-            else:
-                fn(s, j)
-            if kind == "acc" and s == PAIRS - 1 and j == 1:
-                finish(1)
-
-        stages = {
-            "widen": widen, "tr1": tr1, "co1": co1, "quant_m": quant_m, "mx1": mx1, "silu1": silu1,
-            "pool": pool_share, "sshare": scalar_share, "outer": outer, "tr2": tr2, "co2": co2,
-            "quant_p": quant_p, "mx2": mx2, "silu2": silu2, "acc": accumulate,
-        }
-        order = [('outer', 0, 0), ('outer', 0, 1), ('co2', -1, 0), ('silu2', -3, 1), ('widen', 5, 0), ('mx2', -2, 1), ('quant_m', 3, None), ('silu1', 2, None), ('sshare', 1, 1), ('co2', -1, 1), ('pool', 2, None), ('tr1', 4, None), ('tr2', 0, 0), ('acc', -3, 1), ('sshare', 1, 0), ('mx1', 3, None), ('tr2', 0, 1), ('quant_p', -1, None), ('widen', 5, 1), ('silu2', -2, 0), ('mx2', -1, 0), ('co1', 4, None), ('acc', -2, 0)]
-        for s in range(-8, PAIRS + 6):
-            for kind, off, j in order:
-                if 0 <= s + off < PAIRS:
-                    pair_stage(kind, s + off, j)
+            run(add_up, s - 3, 0)
+            run(add_up, s - 3, 1)
+            run(turn_p, s, 1)
+            run(basis_product, s + 1, 1)
+            run(copy_m, s + 4)
+            run(copy_p, s, 0)
+            run(quantise_m, s + 3)
+            if s == -3:
+                permute_w_down()
+            run(multiply_down, s + 3)
+            run(quantise_p, s - 1)
+            run(multiply_bil, s - 1, 0)
+        finish(1)

from contextlib import ExitStack

import concourse.mybir as mybir
from concourse.masks import make_identity

F32 = mybir.dt.float32
BF16 = mybir.dt.bfloat16
I32 = mybir.dt.int32
U8 = mybir.dt.uint8
FP8 = mybir.dt.float8_e4m3fn
FP8X4 = mybir.dt.float8_e4m3fn_x4
ACT = mybir.ActivationFunctionType
ALU = mybir.AluOpType

P = 128
E, K, D, C, NB = 256, 16, 512, 128, 8
NBC = NB * C
FLOPS = 2 * E * K * D * C + 2 * E * K * NBC * D

PAIRS = E * K // (2 * P)
PAIRS_PER_BLOCK = K // 2
MAX_SHARE = 3
PREFETCH = 5
CHUNKS = (2, 2, 4, 4, 4, 4, 4, 4, 4)


def share(s):
    if s >= PAIRS - 3:
        return 1
    return 3 if s % 3 == 0 else 2


def tile_dimenettripletbilinear_w8_kernel(
    tc, m_kj_bytes, m_kj_scale, m_ji, sbf, w_down_words, w_down_scales, gain, w_bil_words, w_bil_scales, out
):
    nc = tc.nc
    with ExitStack() as ctx:
        keep = ctx.enter_context(tc.tile_pool(name="keep", bufs=1))
        work = ctx.enter_context(tc.tile_pool(name="work", bufs=3))
        psum = ctx.enter_context(tc.psum_pool(name="psum", bufs=1))
        ctx.enter_context(tc.manual_schedule())

        scale_cols = keep.tile([P, 4], F32, name="scale_cols", align_bytes=64)
        scale = keep.tile([P, D], F32, name="scale", align_bytes=64)
        down_raw = keep.tile([P, C], I32, name="down_raw", align_bytes=64)
        down_scales_raw = keep.tile([P, C], U8, name="down_scales_raw", align_bytes=64)
        down = keep.tile([P, C], I32, name="down", align_bytes=64)
        down_scales = keep.tile([P, C], U8, name="down_scales", align_bytes=64)
        bil = keep.tile([P, 2, D], I32, name="bil", align_bytes=64)
        bil_scales = keep.tile([P, D], U8, name="bil_scales", align_bytes=64)
        basis = keep.tile([P, 2, K * NB], BF16, name="basis", align_bytes=64)
        basis_f32 = keep.tile([P, 2, K * NB], F32, name="basis_f32", align_bytes=64)
        residual = keep.tile([P, 2, D], BF16, name="residual", align_bytes=64)
        gain_row = keep.tile([P, NBC], BF16, name="gain_row", align_bytes=64)
        gain_shared = keep.tile([P, MAX_SHARE, C], BF16, name="gain_shared", align_bytes=64)
        ones = keep.tile([P, P], BF16, name="ones", align_bytes=64)
        ident = keep.tile([P, P], F32, name="ident", align_bytes=64)
        first_silu = keep.tile([P, 1], F32, name="first_silu", align_bytes=64)
        gain_all = psum.tile([P, 2, 2, 256], BF16, name="gain_all")

        nc.gpsimd.memset(first_silu[:], 0.0)
        make_identity(nc, ident[:])
        nc.gpsimd.memset(ones[:], 1.0)
        nc.vector.memset(down_scales_raw[:].bitcast(I32), 0)
        nc.vector.memset(bil_scales[:].bitcast(I32), 0)
        nc.vector.memset(gain_row[:], 0.0)

        byte_rows = []

        def load_bytes(k_count):
            b, k0 = divmod(len(byte_rows), K)
            chunk = keep.tile([P, k_count * D], U8, name="bytes_%d_%d" % (b, k0), align_bytes=64)
            nc.sync.dma_start(
                out=chunk[:], in_=m_kj_bytes[b * P : (b + 1) * P, k0 : k0 + k_count, :].rearrange("e k d -> e (k d)")
            )
            byte_rows.extend([chunk[:, j * D : (j + 1) * D] for j in range(k_count)])

        nc.sync.dma_start(out=scale_cols[:], in_=m_kj_scale.rearrange("a b (p t) -> p (a b t)", t=4))
        load_bytes(CHUNKS[0])
        for quad in range(4):
            nc.sync.dma_start(
                out=down_scales_raw[32 * quad : 32 * quad + 4, :].bitcast(I32),
                in_=w_down_scales[0, 4 * quad : 4 * quad + 4, :].bitcast(I32),
            )
        nc.sync.dma_start(out=down_raw[:], in_=w_down_words[0].rearrange("p n t -> p (n t)").bitcast(I32))
        for k_count in CHUNKS[1:]:
            load_bytes(k_count)
        for g in range(2):
            nc.sync.dma_start(out=bil[:, g, :], in_=w_bil_words[g].rearrange("p n t -> p (n t)").bitcast(I32))
        for quad in range(4):
            nc.sync.dma_start(
                out=bil_scales[32 * quad : 32 * quad + 8, :].bitcast(I32),
                in_=w_bil_scales[:, 4 * quad : 4 * quad + 4, :].bitcast(I32),
            )
        nc.scalar.dma_start(out=gain_row[0:1, :], in_=gain.rearrange("(o k) -> o k", o=1))
        nc.scalar.dma_start(out=basis[:], in_=sbf.rearrange("(b e) k n -> e b (k n)", b=2))
        nc.scalar.dma_start(out=residual[:], in_=m_ji.rearrange("(b e) d -> e b d", b=2))

        nc.scalar.activation(out=first_silu[:], in_=first_silu[:], func=ACT.Silu)

        spread = psum.tile([P, 4, P], F32, name="words2", bufs=2)
        for t in range(4):
            nc.tensor.transpose(spread[:, t, :], scale_cols[:, t : t + 1].to_broadcast([P, P]), ident[:])
        nc.vector.tensor_copy(out=scale[:].rearrange("p (k t) -> p k t", t=4), in_=spread[:].rearrange("p t k -> p k t"))

        def fill_gain():
            for g in range(2):
                nc.tensor.matmul(
                    out=gain_all[:, g].rearrange("p u (m e) -> p u m e", e=2),
                    lhsT=ones[:],
                    rhs=gain_row[:, g * 512 : (g + 1) * 512].rearrange("p (m u e) -> p u m e", u=2, e=2),
                    start=True,
                    stop=True,
                )

        def prepare_sharing():
            nc.vector.tensor_copy(out=basis_f32[:], in_=basis[:])
            for i in range(MAX_SHARE):
                g, h = divmod(NB - MAX_SHARE + i, 4)
                nc.vector.tensor_copy(
                    out=gain_shared[:, i, :].rearrange("p (u c) -> p u c", u=2),
                    in_=gain_all[:, g, :, 64 * h : 64 * h + 64],
                )

        def permute_w_down():
            for dst, src in ((down, down_raw), (down_scales, down_scales_raw)):
                nc.vector.tensor_copy(
                    out=dst[:].rearrange("p (u q e) -> p q u e", u=2, q=32),
                    in_=src[:].rearrange("p (q u e) -> p q u e", u=2, q=32),
                )

        tiles = {}

        def widen(s, j):
            if j == 0:
                tiles["m", s] = work.tile([P, 2, D], BF16, name="m", align_bytes=64)
            nc.vector.tensor_tensor(
                out=tiles["m", s][:, j, :], in0=byte_rows[2 * s + j].bitcast(FP8), in1=scale[:], op=ALU.mult
            )

        def turn_m(s):
            words1 = psum.tile([P, 2, 2, P], F32, name="words1")
            tiles["words1", s] = words1
            words = tiles["m", s][:].rearrange("p j k -> p (j k)").bitcast(F32)
            for j in range(2):
                for u in range(2):
                    nc.tensor.transpose(words1[:, j, u, :], words[:, 256 * j + u : 256 * (j + 1) : 2], ident[:])

        def copy_m(s):
            m_t = work.tile([P, 2 * P * 4], BF16, name="m_t", align_bytes=64)
            tiles["m_t", s] = m_t
            nc.scalar.copy(
                out=m_t[:].bitcast(F32).rearrange("p (j r u) -> p j r u", j=2, u=2),
                in_=tiles["words1", s][:].rearrange("p j u r -> p j r u"),
            )

        def quantise_m(s):
            codes = work.tile([P, 2 * P], I32, name="m_codes", align_bytes=64)
            scales = work.tile([P, 2 * P], U8, name="m_scales", align_bytes=64)
            tiles["mq", s] = (codes, scales)
            nc.vector.quantize_mx(out=codes[:].bitcast(FP8X4), scales=scales[:], in_=tiles["m_t", s][:])

        def multiply_down(s):
            y = psum.tile([P, 2, C], F32, name="y")
            tiles["y", s] = y
            codes, scales = tiles["mq", s]
            for j in range(2):
                rows = slice(j * P, (j + 1) * P)
                nc.tensor.matmul_mx(
                    out=y[:, j, :],
                    lhsT=codes[:, rows].bitcast(FP8X4),
                    lhsT_scale=scales[:, rows],
                    rhs=down[:].bitcast(FP8X4),
                    rhs_scale=down_scales[:],
                    start=True,
                    stop=True,
                )

        def silu_x(s):
            x = work.tile([P, 2, C], F32, name="x", align_bytes=64)
            tiles["x", s] = x
            nc.scalar.activation(out=x[:], in_=tiles["y", s][:], func=ACT.Silu)

        def gain_product(s):
            xg = work.tile([P, 2, MAX_SHARE, C], F32, name="xg", align_bytes=64)
            tiles["xg", s] = xg
            m = share(s)
            nc.gpsimd.tensor_tensor(
                out=xg[:, :, MAX_SHARE - m :, :],
                in0=tiles["x", s][:].unsqueeze(2).to_broadcast([P, 2, m, C]),
                in1=gain_shared[:, MAX_SHARE - m :, :].unsqueeze(1).to_broadcast([P, 2, m, C]),
                op=ALU.mult,
            )

        def basis_product(s, j):
            prod = work.tile([P, 2, 2, 256], BF16, name="prod", bufs=6, align_bytes=64)
            tiles["prod", s, j] = prod
            b, k = divmod(2 * s + j, K)
            for n in range(NB - share(s), NB):
                g, h = divmod(n, 4)
                nc.scalar.activation(
                    out=prod[:, g, :, 64 * h : 64 * h + 64],
                    in_=tiles["xg", s][:, j, n - NB + MAX_SHARE, :].rearrange("p (u c) -> p u c", u=2),
                    func=ACT.Copy,
                    scale=basis_f32[:, b, k * NB + n : k * NB + n + 1],
                )

        def outer(s, j):
            prod = tiles["prod", s, j]
            b, k = divmod(2 * s + j, K)
            for n in range(NB - share(s)):
                g, h = divmod(n, 4)
                cols = slice(64 * h, 64 * h + 64)
                nc.vector.scalar_tensor_tensor(
                    out=prod[:, g, :, cols],
                    in0=tiles["x", s][:, j, :].rearrange("p (u c) -> p u c", u=2),
                    scalar=basis[:, b, k * NB + n : k * NB + n + 1],
                    in1=gain_all[:, g, :, cols],
                    op0=ALU.mult,
                    op1=ALU.mult,
                )

        def turn_p(s, j):
            words2 = psum.tile([P, 4, P], F32, name="words2", bufs=2)
            tiles["words2", s, j] = words2
            words = tiles["prod", s, j][:].rearrange("p g u c -> p (g u c)").bitcast(F32)
            for gu in range(4):
                nc.tensor.transpose(words2[:, gu, :], words[:, P * gu : P * (gu + 1)], ident[:])

        def copy_p(s, j):
            if j == 0:
                tiles["p_t", s] = work.tile([P, 2 * 2 * P * 4], BF16, name="p_t", align_bytes=64)
            words = tiles["p_t", s][:].bitcast(F32).rearrange("p (g r u) -> p g r u", g=2, u=2)
            nc.scalar.copy(
                out=words[:, :, j * P : (j + 1) * P, :],
                in_=tiles["words2", s, j][:].rearrange("p (g u) r -> p g r u", g=2),
            )

        def quantise_p(s):
            codes = work.tile([P, 2 * 2 * P], I32, name="p_codes", align_bytes=64)
            scales = work.tile([P, 2 * 2 * P], U8, name="p_scales", align_bytes=64)
            tiles["pq", s] = (codes, scales)
            nc.vector.quantize_mx(out=codes[:].bitcast(FP8X4), scales=scales[:], in_=tiles["p_t", s][:])

        def multiply_bil(s, half):
            z = psum.tile([P, 2, 2 * P], F32, name="z", bufs=2)
            tiles["z", s, half] = z
            codes, scales = tiles["pq", s]
            for i in range(2):
                d_cols = slice((2 * half + i) * P, (2 * half + i + 1) * P)
                for g in range(2):
                    rows = slice(2 * P * g, 2 * P * (g + 1))
                    nc.tensor.matmul_mx(
                        out=z[:, i, :],
                        lhsT=bil[:, g, d_cols].bitcast(FP8X4),
                        lhsT_scale=bil_scales[4 * g : P, d_cols],
                        rhs=codes[:, rows].bitcast(FP8X4),
                        rhs_scale=scales[:, rows],
                        start=(g == 0),
                        stop=(g == 1),
                    )

        def silu_t(s, half):
            t = work.tile([P, 2, 2 * P], F32, name="t", bufs=4, align_bytes=64)
            tiles["t", s, half] = t
            nc.scalar.activation(out=t[:], in_=tiles["z", s, half][:], func=ACT.Silu)

        def add_up(s, half):
            b, pair = divmod(s, PAIRS_PER_BLOCK)
            first, last = pair == 0 and half == 0, pair == PAIRS_PER_BLOCK - 1 and half == 1
            if first:
                tiles["sum", b] = psum.tile([P, D], F32, name="sum")
            for i in range(2):
                d0 = (2 * half + i) * P
                for j in range(2):
                    nc.tensor.matmul(
                        out=tiles["sum", b][:, d0 : d0 + P],
                        lhsT=tiles["t", s, half][:, i, j * P : (j + 1) * P],
                        rhs=ident[:],
                        is_transpose=True,
                        start=(first and i == 0 and j == 0),
                        stop=(last and i == 1 and j == 1),
                    )

        def finish(b):
            for half in range(2):
                cols = slice(256 * half, 256 * (half + 1))
                o = work.tile([P, 256], F32, name="o", bufs=4, align_bytes=64)
                nc.vector.scalar_tensor_tensor(
                    out=o[:],
                    in0=tiles["sum", b][:, cols],
                    scalar=0.25,
                    in1=residual[:, b, cols],
                    op0=ALU.mult,
                    op1=ALU.add,
                )
                nc.sync.dma_start(out=out[b * P : (b + 1) * P, cols], in_=o[:])

        def run(stage, s, *part):
            if 0 <= s < PAIRS:
                stage(s, *part)

        for s in range(-PREFETCH, PAIRS + 3):
            run(widen, s + PREFETCH, 0)
            run(widen, s + PREFETCH, 1)
            if s == -2:
                prepare_sharing()
            run(copy_p, s - 1, 1)
            run(silu_x, s + 2)
            run(gain_product, s + 2)
            run(basis_product, s + 1, 0)
            run(outer, s, 0)
            run(outer, s, 1)
            run(multiply_bil, s - 2, 1)
            run(silu_t, s - 2, 0)
            run(silu_t, s - 2, 1)
            if s == -3:
                fill_gain()
            run(turn_m, s + 4)
            run(turn_p, s, 0)
            if s - 3 == PAIRS_PER_BLOCK:
                finish(0)
            run(add_up, s - 3, 0)
            run(add_up, s - 3, 1)
            run(turn_p, s, 1)
            run(basis_product, s + 1, 1)
            run(copy_m, s + 4)
            run(copy_p, s, 0)
            run(quantise_m, s + 3)
            if s == -3:
                permute_w_down()
            run(multiply_down, s + 3)
            run(quantise_p, s - 1)
            run(multiply_bil, s - 1, 0)
        finish(1)
